import numpy as np
import ml_dtypes


def mxq(x, axis, fmt="e4m3"):
    dtype, down = {"e4m3": (ml_dtypes.float8_e4m3fn, 7), "e5m2": (ml_dtypes.float8_e5m2, 14)}[fmt]
    v = np.moveaxis(np.asarray(x, np.float32).astype(ml_dtypes.bfloat16).astype(np.float64), axis, -1)
    blocks = v.reshape(v.shape[:-1] + (-1, 32))
    amax = np.abs(blocks).max(-1, keepdims=True)
    byte = np.maximum(np.where(amax > 0, np.frexp(amax)[1] - 1 + 127, 0) - down, 1)
    scale = np.exp2(byte - 127.0)
    codes = (blocks / scale).astype(np.float32).astype(dtype).astype(np.float64)
    return np.moveaxis((codes * scale).reshape(v.shape), -1, axis)


WIDE = False


def mx_kscale(k):
    if not WIDE:
        return np.ones(k)
    levels = np.array([10, -10, 5, -5, 0])
    if k % 512:
        return np.exp2(np.random.permutation(np.resize(levels, k // 32))).repeat(32)
    a = np.empty((k // 512, 16))
    for p in range(k // 512):
        a[p, :8] = np.random.permutation(np.resize(levels, 8))
        for g in range(8):
            far = levels[np.abs(levels - a[p, g]) >= 10]
            a[p, g + 8] = far[np.random.randint(len(far))]
    return np.exp2(a.ravel()).repeat(32)


def f64(x):
    return np.asarray(x).astype(np.float64)


def striped(idx):
    return np.tile(np.asarray(idx).reshape(-1, 16).T, (8, 1)).astype(np.uint16)


def unstriped(offs):
    return offs[:16].T.reshape(-1).astype(np.int64)


G, K, T, D, M = 64, 16, 2048, 512, 256


def setup_inputs():
    n = np.random.standard_normal
    s = mx_kscale(D)[:, None]
    x = n((D, T)) * s
    idx = np.stack([np.random.permutation(T)[:K] for g in range(G)])
    return {
        "xT": x.astype(np.float32),
        "w": (n((D, M)) / np.sqrt(D) / s).astype(np.float32),
        "offs": striped(idx.reshape(-1)),
    }


def reference(xT, w, offs):
    x = f64(xT)[:, unstriped(offs)]
    y = (mxq(f64(w), 0, "e4m3").T @ mxq(x, 0, "e4m3")).reshape(M, G, K).max(-1)
    return y

@@ -1,0 +1,172 @@
+from contextlib import ExitStack
+
+import concourse.mybir as mybir
+from concourse.masks import make_identity
+
+D, T, M = 512, 2048, 256
+G, NB = 64, 16
+E = G * NB
+P = 128
+FLOPS = 2 * D * M * E
+
+F32 = mybir.dt.float32
+BF16 = mybir.dt.bfloat16
+U32 = mybir.dt.uint32
+U16 = mybir.dt.uint16
+U8 = mybir.dt.uint8
+FP8X4 = mybir.dt.float8_e4m3fn_x4
+COPY = mybir.ActivationFunctionType.Copy
+MAX = mybir.AluOpType.max
+AXIS_X = mybir.AxisListType.X
+
+HALVES = 2
+EH = E // HALVES
+GH = G // HALVES
+PIECES = [(0, 256), (256, 256), (512, 256), (768, 256)]
+
+
+def tile_attend_edge_kernel(tc, xT, w, offs, out):
+    nc = tc.nc
+    x_rows = xT.rearrange("(p j) t -> p j t", j=4)
+    w_rows = w.rearrange("(p j) m -> p j m", j=4)
+    out_rows = out.rearrange("(a p) g -> p a g", p=P)
+
+    with ExitStack() as ctx:
+        keep = ctx.enter_context(tc.tile_pool(name="keep", bufs=1))
+        psum = ctx.enter_context(tc.psum_pool(name="psum", bufs=1))
+
+        lists = keep.tile([P, E // 16], U16, name="lists")
+        nc.sync.dma_start(lists[:], offs)
+        tables = [keep.tile([P, T], F32, name=f"table{t}") for t in range(4)]
+        for t in range(4):
+            nc.sync.dma_start(tables[t][:], x_rows[:, t, :])
+        w_raw = keep.tile([P, 4, M], F32, name="w_raw")
+        nc.sync.dma_start(w_raw[:], w_rows)
+
+        dense = [keep.tile([P, 2, E], F32, name=f"dense{u}") for u in range(2)]
+        cols = [keep.tile([P, EH, 4], BF16, name=f"cols{h}", align_bytes=64) for h in range(HALVES)]
+
+        def gather(t, first, n):
+            u, e = divmod(t, 2)
+            nc.vector.tensor_copy(
+                dense[u][:, e, first : first + n], tables[t][:].indirect(lists[:, first // 16 : (first + n) // 16])
+            )
+
+        def weave(u, first, n):
+            h, c = divmod(first, EH)
+            nc.scalar.copy(
+                cols[h][:, c : c + n, 2 * u : 2 * u + 2], dense[u][:, :, first : first + n].rearrange("p e c -> p c e")
+            )
+
+        identity = keep.tile([P, P], F32, name="identity")
+        make_identity(nc, identity[:])
+        spare = psum.tile([P, P], F32, name="spare")
+
+        def warm(first, times):
+            for k in range(times):
+                nc.tensor.transpose(spare[:], dense[1][:, 1, first : first + P], identity[:])
+
+        w_bf = [keep.tile([P, P, 4], BF16, name=f"w_bf{a}", tag=f"shared{a}", align_bytes=64) for a in range(M // P)]
+        w_codes = [keep.tile([P, P], U32, name=f"w_codes{a}", align_bytes=64) for a in range(M // P)]
+        w_scales = [keep.tile([P, P], U8, name=f"w_scales{a}", align_bytes=64) for a in range(M // P)]
+
+        def cast_w(a):
+            nc.gpsimd.tensor_scalar(
+                w_bf[a][:],
+                w_raw[:, :, a * P : (a + 1) * P].rearrange("p j m -> p m j"),
+                1.0,
+                0.0,
+                mybir.AluOpType.mult,
+                mybir.AluOpType.add,
+            )
+
+        def quantize_w(a):
+            nc.vector.quantize_mx(
+                out=w_codes[a][:].bitcast(FP8X4), scales=w_scales[a][:], in_=w_bf[a][:].rearrange("p m j -> p (m j)")
+            )
+
+        codes = [keep.tile([P, n], U32, name=f"codes{i}", align_bytes=64) for i, (first, n) in enumerate(PIECES)]
+        scales = [None] * len(PIECES)
+        sums = {}
+
+        def quantize(i):
+            first, n = PIECES[i]
+            h, c = divmod(first, EH)
+            shared = {0: "shared2", 1: "shared0", 2: "shared1", 3: "shared2"}
+            scales[i] = keep.tile([P, n], U8, name=f"scales{i}", tag=shared.get(i, f"scales{i}"), align_bytes=64)
+            nc.vector.quantize_mx(
+                out=codes[i][:].bitcast(FP8X4),
+                scales=scales[i][:],
+                in_=cols[h][:].rearrange("p c j -> p (c j)")[:, 4 * c : 4 * (c + n)],
+            )
+
+        def multiply(i, a):
+            first, n = PIECES[i]
+            if a == 0:
+                sums[i] = psum.tile([P, M // P, n], F32, name=f"bank{i}")
+            nc.tensor.matmul_mx(
+                out=sums[i][:, a, :],
+                lhsT=w_codes[a][:].bitcast(FP8X4),
+                lhsT_scale=w_scales[a][:],
+                rhs=codes[i][:].bitcast(FP8X4),
+                rhs_scale=scales[i][:],
+                start=True,
+                stop=True,
+            )
+
+        ys = [keep.tile([P, M // P, GH], F32, name=f"y{h}") for h in range(HALVES)]
+
+        def largest(i):
+            first, n = PIECES[i]
+            h, c = divmod(first, EH)
+            nc.vector.tensor_reduce(
+                ys[h][:, :, c // NB : (c + n) // NB],
+                sums[i][:].rearrange("p a (g j) -> p a g j", j=NB),
+                AXIS_X,
+                MAX,
+            )
+
+        def store(h):
+            nc.sync.dma_start(out_rows[:, :, h * GH : (h + 1) * GH], ys[h][:])
+
+        for h in range(HALVES):
+            gather(0, h * EH, EH)
+        for h in range(HALVES):
+            gather(1, h * EH, EH)
+        for h in range(HALVES):
+            weave(0, h * EH, EH)
+        for h in range(HALVES):
+            gather(2, h * EH, EH)
+        gather(3, 0, 256)
+        weave(1, 0, 256)
+        gather(3, 256, 256)
+        weave(1, 256, 256)
+        warm(256, 5)
+        gather(3, 512, 256)
+        weave(1, 512, 256)
+        warm(512, 5)
+        gather(3, 768, 256)
+        weave(1, 768, 256)
+        warm(768, 3)
+        cast_w(0)
+        cast_w(1)
+        quantize(0)
+        quantize_w(0)
+        multiply(0, 0)
+        quantize(1)
+        multiply(1, 0)
+        quantize_w(1)
+        multiply(0, 1)
+        multiply(1, 1)
+        quantize(2)
+        multiply(2, 0)
+        multiply(2, 1)
+        largest(0)
+        quantize(3)
+        multiply(3, 0)
+        multiply(3, 1)
+        largest(1)
+        store(0)
+        largest(2)
+        largest(3)
+        store(1)

@@ -1,7 +1,6 @@
 from contextlib import ExitStack
 
 import concourse.mybir as mybir
-from concourse.masks import make_identity
 
 D, T, M = 512, 2048, 256
 G, NB = 64, 16
@@ -11,6 +10,7 @@ FLOPS = 2 * D * M * E
 
 F32 = mybir.dt.float32
 BF16 = mybir.dt.bfloat16
+I32 = mybir.dt.int32
 U32 = mybir.dt.uint32
 U16 = mybir.dt.uint16
 U8 = mybir.dt.uint8
@@ -19,10 +19,13 @@ COPY = mybir.ActivationFunctionType.Copy
 MAX = mybir.AluOpType.max
 AXIS_X = mybir.AxisListType.X
 
-HALVES = 2
-EH = E // HALVES
-GH = G // HALVES
-PIECES = [(0, 256), (256, 256), (512, 256), (768, 256)]
+N = 256
+PIECES = E // N
+FIRST = 512
+LOAD_ORDER = [2, 0, 1, 3]
+CHUNKS = [(0, 1280), (1280, 768)]
+LAST_CHUNKS = [(0, 1280), (1280, 512), (1792, 256)]
+SHARE = {0: 384, 1: 384, 2: N, 3: N}
 
 
 def tile_attend_edge_kernel(tc, xT, w, offs, out):
@@ -36,137 +39,102 @@ def tile_attend_edge_kernel(tc, xT, w, offs, out):
         psum = ctx.enter_context(tc.psum_pool(name="psum", bufs=1))
 
         lists = keep.tile([P, E // 16], U16, name="lists")
-        nc.sync.dma_start(lists[:], offs)
         tables = [keep.tile([P, T], F32, name=f"table{t}") for t in range(4)]
-        for t in range(4):
-            nc.sync.dma_start(tables[t][:], x_rows[:, t, :])
-        w_raw = keep.tile([P, 4, M], F32, name="w_raw")
+        narrow = [keep.tile([P, T], BF16, name=f"narrow{t}") for t in range(4)]
+        w_raw = keep.tile([P, 4, M], F32, name="w_raw", tag="slot1", align_bytes=64)
+        cols = keep.tile([P, E * 4], BF16, name="cols", align_bytes=64)
+        places = cols[:].rearrange("p (c j) -> p c j", j=4)
+
+        for t in LOAD_ORDER:
+            for c, n in LAST_CHUNKS if t == 3 else CHUNKS:
+                nc.sync.dma_start(tables[t][:, c : c + n], x_rows[:, t, c : c + n])
+                if t == LOAD_ORDER[0] and c == 0:
+                    nc.sync.dma_start(lists[:], offs)
         nc.sync.dma_start(w_raw[:], w_rows)
 
-        dense = [keep.tile([P, 2, E], F32, name=f"dense{u}") for u in range(2)]
-        cols = [keep.tile([P, EH, 4], BF16, name=f"cols{h}", align_bytes=64) for h in range(HALVES)]
-
-        def gather(t, first, n):
-            u, e = divmod(t, 2)
+        def gather_vector(t, first, n):
             nc.vector.tensor_copy(
-                dense[u][:, e, first : first + n], tables[t][:].indirect(lists[:, first // 16 : (first + n) // 16])
+                places[:, first : first + n, t], tables[t][:].indirect(lists[:, first // 16 : (first + n) // 16])
             )
 
-        def weave(u, first, n):
-            h, c = divmod(first, EH)
-            nc.scalar.copy(
-                cols[h][:, c : c + n, 2 * u : 2 * u + 2], dense[u][:, :, first : first + n].rearrange("p e c -> p c e")
+        def gather_scalar(t, first, n):
+            nc.scalar.activation(
+                places[:, first : first + n, t], narrow[t][:].indirect(lists[:, first // 16 : (first + n) // 16]), COPY
             )
 
-        identity = keep.tile([P, P], F32, name="identity")
-        make_identity(nc, identity[:])
-        spare = psum.tile([P, P], F32, name="spare")
+        for t in LOAD_ORDER[:3]:
+            for c, n in CHUNKS:
+                if t == LOAD_ORDER[0] and c == 0:
+                    nc.scalar.copy(narrow[t][:, :FIRST], tables[t][:, :FIRST])
+                    nc.vector.tensor_copy(narrow[t][:, FIRST:n], tables[t][:, FIRST:n])
+                else:
+                    nc.vector.tensor_copy(narrow[t][:, c : c + n], tables[t][:, c : c + n])
+            gather_vector(t, 0, SHARE[t])
+            gather_scalar(t, SHARE[t], E - SHARE[t])
+        for c, n in LAST_CHUNKS[:-1]:
+            nc.vector.tensor_copy(narrow[3][:, c : c + n], tables[3][:, c : c + n])
+        c, n = LAST_CHUNKS[-1]
+        nc.scalar.copy(narrow[3][:, c : c + n], tables[3][:, c : c + n])
+        gather_vector(3, 0, N)
+        for i in range(1, PIECES):
+            gather_scalar(3, i * N, N)
 
-        def warm(first, times):
-            for k in range(times):
-                nc.tensor.transpose(spare[:], dense[1][:, 1, first : first + P], identity[:])
+        w_bf = keep.tile([P, M, 4], BF16, name="w_bf", tag="slot2", align_bytes=64)
+        w_codes = keep.tile([P, M], U32, name="w_codes", align_bytes=64)
+        w_scales = keep.tile([P, M], U8, name="w_scales", align_bytes=64)
 
-        w_bf = [keep.tile([P, P, 4], BF16, name=f"w_bf{a}", tag=f"shared{a}", align_bytes=64) for a in range(M // P)]
-        w_codes = [keep.tile([P, P], U32, name=f"w_codes{a}", align_bytes=64) for a in range(M // P)]
-        w_scales = [keep.tile([P, P], U8, name=f"w_scales{a}", align_bytes=64) for a in range(M // P)]
+        def cast_w():
+            nc.vector.tensor_copy(w_bf[:], w_raw[:].rearrange("p j m -> p m j"))
 
-        def cast_w(a):
-            nc.gpsimd.tensor_scalar(
-                w_bf[a][:],
-                w_raw[:, :, a * P : (a + 1) * P].rearrange("p j m -> p m j"),
-                1.0,
-                0.0,
-                mybir.AluOpType.mult,
-                mybir.AluOpType.add,
-            )
-
-        def quantize_w(a):
+        def quantize_w():
             nc.vector.quantize_mx(
-                out=w_codes[a][:].bitcast(FP8X4), scales=w_scales[a][:], in_=w_bf[a][:].rearrange("p m j -> p (m j)")
+                out=w_codes[:].bitcast(FP8X4), scales=w_scales[:], in_=w_bf[:].rearrange("p m j -> p (m j)")
             )
 
-        codes = [keep.tile([P, n], U32, name=f"codes{i}", align_bytes=64) for i, (first, n) in enumerate(PIECES)]
-        scales = [None] * len(PIECES)
-        sums = {}
-
-        def quantize(i):
-            first, n = PIECES[i]
-            h, c = divmod(first, EH)
-            shared = {0: "shared2", 1: "shared0", 2: "shared1", 3: "shared2"}
-            scales[i] = keep.tile([P, n], U8, name=f"scales{i}", tag=shared.get(i, f"scales{i}"), align_bytes=64)
-            nc.vector.quantize_mx(
-                out=codes[i][:].bitcast(FP8X4),
-                scales=scales[i][:],
-                in_=cols[h][:].rearrange("p c j -> p (c j)")[:, 4 * c : 4 * (c + n)],
-            )
+        codes = [keep.tile([P, N], U32, name=f"codes{i}", align_bytes=64) for i in range(PIECES)]
+        scales = [None] * PIECES
+        slots = ["slot0", "slot1", "slot2", "slot0"]
+        sums = [psum.tile([P, M // P, N], F32, name=f"bank{i}") for i in range(PIECES)]
 
         def multiply(i, a):
-            first, n = PIECES[i]
-            if a == 0:
-                sums[i] = psum.tile([P, M // P, n], F32, name=f"bank{i}")
             nc.tensor.matmul_mx(
                 out=sums[i][:, a, :],
-                lhsT=w_codes[a][:].bitcast(FP8X4),
-                lhsT_scale=w_scales[a][:],
+                lhsT=w_codes[:, a * P : (a + 1) * P].bitcast(FP8X4),
+                lhsT_scale=w_scales[:, a * P : (a + 1) * P],
                 rhs=codes[i][:].bitcast(FP8X4),
                 rhs_scale=scales[i][:],
                 start=True,
                 stop=True,
             )
 
-        ys = [keep.tile([P, M // P, GH], F32, name=f"y{h}") for h in range(HALVES)]
+        GH = G // 2
+        ys = [keep.tile([P, M // P, GH], F32, name=f"y{h}") for h in range(2)]
 
         def largest(i):
-            first, n = PIECES[i]
-            h, c = divmod(first, EH)
+            h, c = divmod(i * N // NB, GH)
             nc.vector.tensor_reduce(
-                ys[h][:, :, c // NB : (c + n) // NB],
-                sums[i][:].rearrange("p a (g j) -> p a g j", j=NB),
-                AXIS_X,
-                MAX,
+                ys[h][:, :, c : c + N // NB], sums[i][:].rearrange("p a (g j) -> p a g j", j=NB), AXIS_X, MAX
             )
 
         def store(h):
             nc.sync.dma_start(out_rows[:, :, h * GH : (h + 1) * GH], ys[h][:])
 
-        for h in range(HALVES):
-            gather(0, h * EH, EH)
-        for h in range(HALVES):
-            gather(1, h * EH, EH)
-        for h in range(HALVES):
-            weave(0, h * EH, EH)
-        for h in range(HALVES):
-            gather(2, h * EH, EH)
-        gather(3, 0, 256)
-        weave(1, 0, 256)
-        gather(3, 256, 256)
-        weave(1, 256, 256)
-        warm(256, 5)
-        gather(3, 512, 256)
-        weave(1, 512, 256)
-        warm(512, 5)
-        gather(3, 768, 256)
-        weave(1, 768, 256)
-        warm(768, 3)
-        cast_w(0)
-        cast_w(1)
+        def quantize(i):
+            scales[i] = keep.tile([P, N], U8, name=f"scales{i}", tag=slots[i], align_bytes=64)
+            nc.vector.quantize_mx(
+                out=codes[i][:].bitcast(FP8X4), scales=scales[i][:], in_=cols[:, 4 * N * i : 4 * N * (i + 1)]
+            )
+
         quantize(0)
-        quantize_w(0)
-        multiply(0, 0)
+        cast_w()
+        quantize_w()
         quantize(1)
-        multiply(1, 0)
-        quantize_w(1)
-        multiply(0, 1)
-        multiply(1, 1)
         quantize(2)
-        multiply(2, 0)
-        multiply(2, 1)
-        largest(0)
-        quantize(3)
-        multiply(3, 0)
-        multiply(3, 1)
-        largest(1)
-        store(0)
-        largest(2)
-        largest(3)
-        store(1)
+        for i in range(PIECES):
+            multiply(i, 0)
+            multiply(i, 1)
+            largest(i)
+            if i == 0:
+                quantize(3)
+            if i % 2 == 1:
+                store(i // 2)

@@ -21,11 +21,10 @@ AXIS_X = mybir.AxisListType.X
 
 N = 256
 PIECES = E // N
-FIRST = 512
-LOAD_ORDER = [2, 0, 1, 3]
+LOAD_ORDER = [0, 1, 2, 3]
 CHUNKS = [(0, 1280), (1280, 768)]
 LAST_CHUNKS = [(0, 1280), (1280, 512), (1792, 256)]
-SHARE = {0: 384, 1: 384, 2: N, 3: N}
+SHARE = {0: 352, 1: 352, 2: N, 3: N}
 
 
 def tile_attend_edge_kernel(tc, xT, w, offs, out):
@@ -64,9 +63,9 @@ def tile_attend_edge_kernel(tc, xT, w, offs, out):
 
         for t in LOAD_ORDER[:3]:
             for c, n in CHUNKS:
-                if t == LOAD_ORDER[0] and c == 0:
-                    nc.scalar.copy(narrow[t][:, :FIRST], tables[t][:, :FIRST])
-                    nc.vector.tensor_copy(narrow[t][:, FIRST:n], tables[t][:, FIRST:n])
+                if t == LOAD_ORDER[0]:
+                    nc.scalar.copy(narrow[t][:, c : c + n // 96 * 32], tables[t][:, c : c + n // 96 * 32])
+                    nc.vector.tensor_copy(narrow[t][:, c + n // 96 * 32 : c + n], tables[t][:, c + n // 96 * 32 : c + n])
                 else:
                     nc.vector.tensor_copy(narrow[t][:, c : c + n], tables[t][:, c : c + n])
             gather_vector(t, 0, SHARE[t])
@@ -79,26 +78,29 @@ def tile_attend_edge_kernel(tc, xT, w, offs, out):
         for i in range(1, PIECES):
             gather_scalar(3, i * N, N)
 
-        w_bf = keep.tile([P, M, 4], BF16, name="w_bf", tag="slot2", align_bytes=64)
+        w_bf = [keep.tile([P, P, 4], BF16, name=f"w_bf{a}", tag=f"w_bf{a}", align_bytes=64) for a in range(M // P)]
         w_codes = keep.tile([P, M], U32, name="w_codes", align_bytes=64)
         w_scales = keep.tile([P, M], U8, name="w_scales", align_bytes=64)
 
-        def cast_w():
-            nc.vector.tensor_copy(w_bf[:], w_raw[:].rearrange("p j m -> p m j"))
+        def cast_w(a):
+            nc.vector.tensor_copy(w_bf[a][:], w_raw[:, :, a * P : (a + 1) * P].rearrange("p j m -> p m j"))
 
-        def quantize_w():
+        def quantize_w(a):
             nc.vector.quantize_mx(
-                out=w_codes[:].bitcast(FP8X4), scales=w_scales[:], in_=w_bf[:].rearrange("p m j -> p (m j)")
+                out=w_codes[:, a * P : (a + 1) * P].bitcast(FP8X4),
+                scales=w_scales[:, a * P : (a + 1) * P],
+                in_=w_bf[a][:].rearrange("p m j -> p (m j)"),
             )
 
         codes = [keep.tile([P, N], U32, name=f"codes{i}", align_bytes=64) for i in range(PIECES)]
         scales = [None] * PIECES
-        slots = ["slot0", "slot1", "slot2", "slot0"]
-        sums = [psum.tile([P, M // P, N], F32, name=f"bank{i}") for i in range(PIECES)]
+        slots = ["slot0", "w_bf0", "w_bf1", "w_bf0"]
+        apart = {i: [psum.tile([P, N], F32, name=f"bank{i}_{a}") for a in range(M // P)] for i in (0, PIECES - 1)}
+        sums = {i: psum.tile([P, M // P, N], F32, name=f"bank{i}") for i in range(1, PIECES - 1)}
 
         def multiply(i, a):
             nc.tensor.matmul_mx(
-                out=sums[i][:, a, :],
+                out=apart[i][a][:] if i in apart else sums[i][:, a, :],
                 lhsT=w_codes[:, a * P : (a + 1) * P].bitcast(FP8X4),
                 lhsT_scale=w_scales[:, a * P : (a + 1) * P],
                 rhs=codes[i][:].bitcast(FP8X4),
@@ -116,6 +118,12 @@ def tile_attend_edge_kernel(tc, xT, w, offs, out):
                 ys[h][:, :, c : c + N // NB], sums[i][:].rearrange("p a (g j) -> p a g j", j=NB), AXIS_X, MAX
             )
 
+        def largest_apart(i, a):
+            h, c = divmod(i * N // NB, GH)
+            nc.vector.tensor_reduce(
+                ys[h][:, a, c : c + N // NB], apart[i][a][:].rearrange("p (g j) -> p g j", j=NB), AXIS_X, MAX
+            )
+
         def store(h):
             nc.sync.dma_start(out_rows[:, :, h * GH : (h + 1) * GH], ys[h][:])
 
@@ -126,15 +134,25 @@ def tile_attend_edge_kernel(tc, xT, w, offs, out):
             )
 
         quantize(0)
-        cast_w()
-        quantize_w()
+        cast_w(0)
+        cast_w(1)
+        quantize_w(0)
+        quantize_w(1)
         quantize(1)
+        multiply(0, 0)
+        largest_apart(0, 0)
         quantize(2)
-        for i in range(PIECES):
-            multiply(i, 0)
-            multiply(i, 1)
-            largest(i)
-            if i == 0:
-                quantize(3)
-            if i % 2 == 1:
-                store(i // 2)
+        multiply(0, 1)
+        largest_apart(0, 1)
+        for a in range(2):
+            multiply(1, a)
+        largest(1)
+        store(0)
+        quantize(3)
+        for a in range(2):
+            multiply(2, a)
+        largest(2)
+        for a in range(2):
+            multiply(3, a)
+            largest_apart(3, a)
+        store(1)

@@ -22,8 +22,8 @@ AXIS_X = mybir.AxisListType.X
 N = 256
 PIECES = E // N
 LOAD_ORDER = [0, 1, 2, 3]
-CHUNKS = [(0, 1280), (1280, 768)]
-LAST_CHUNKS = [(0, 1280), (1280, 512), (1792, 256)]
+CHUNKS = [(0, 1408), (1408, 640)]
+LAST_CHUNKS = [(0, 1408), (1408, 640)]
 SHARE = {0: 352, 1: 352, 2: N, 3: N}
 
 
@@ -70,10 +70,8 @@ def tile_attend_edge_kernel(tc, xT, w, offs, out):
                     nc.vector.tensor_copy(narrow[t][:, c : c + n], tables[t][:, c : c + n])
             gather_vector(t, 0, SHARE[t])
             gather_scalar(t, SHARE[t], E - SHARE[t])
-        for c, n in LAST_CHUNKS[:-1]:
+        for c, n in LAST_CHUNKS:
             nc.vector.tensor_copy(narrow[3][:, c : c + n], tables[3][:, c : c + n])
-        c, n = LAST_CHUNKS[-1]
-        nc.scalar.copy(narrow[3][:, c : c + n], tables[3][:, c : c + n])
         gather_vector(3, 0, N)
         for i in range(1, PIECES):
             gather_scalar(3, i * N, N)
@@ -83,7 +81,10 @@ def tile_attend_edge_kernel(tc, xT, w, offs, out):
         w_scales = keep.tile([P, M], U8, name="w_scales", align_bytes=64)
 
         def cast_w(a):
-            nc.vector.tensor_copy(w_bf[a][:], w_raw[:, :, a * P : (a + 1) * P].rearrange("p j m -> p m j"))
+            nc.vector.tensor_copy(
+                w_bf[a][:].rearrange("p (c i) j -> p c j i", i=4),
+                w_raw[:, :, a * P : (a + 1) * P].rearrange("p j (c i) -> p c j i", i=4),
+            )
 
         def quantize_w(a):
             nc.vector.quantize_mx(
@@ -94,7 +95,7 @@ def tile_attend_edge_kernel(tc, xT, w, offs, out):
 
         codes = [keep.tile([P, N], U32, name=f"codes{i}", align_bytes=64) for i in range(PIECES)]
         scales = [None] * PIECES
-        slots = ["slot0", "w_bf0", "w_bf1", "w_bf0"]
+        slots = ["slot1", "w_bf0", "w_bf1", "slot1"]
         apart = {i: [psum.tile([P, N], F32, name=f"bank{i}_{a}") for a in range(M // P)] for i in (0, PIECES - 1)}
         sums = {i: psum.tile([P, M // P, N], F32, name=f"bank{i}") for i in range(1, PIECES - 1)}
 
@@ -127,32 +128,34 @@ def tile_attend_edge_kernel(tc, xT, w, offs, out):
         def store(h):
             nc.sync.dma_start(out_rows[:, :, h * GH : (h + 1) * GH], ys[h][:])
 
+        def store_apart(h, a):
+            nc.sync.dma_start(out_rows[:, a, h * GH : (h + 1) * GH], ys[h][:, a, :])
+
         def quantize(i):
             scales[i] = keep.tile([P, N], U8, name=f"scales{i}", tag=slots[i], align_bytes=64)
             nc.vector.quantize_mx(
                 out=codes[i][:].bitcast(FP8X4), scales=scales[i][:], in_=cols[:, 4 * N * i : 4 * N * (i + 1)]
             )
 
-        quantize(0)
         cast_w(0)
         cast_w(1)
         quantize_w(0)
+        quantize(0)
         quantize_w(1)
         quantize(1)
-        multiply(0, 0)
-        largest_apart(0, 0)
         quantize(2)
-        multiply(0, 1)
-        largest_apart(0, 1)
+        for a in range(2):
+            multiply(0, a)
+            largest_apart(0, a)
+        quantize(3)
         for a in range(2):
             multiply(1, a)
         largest(1)
         store(0)
-        quantize(3)
         for a in range(2):
             multiply(2, a)
         largest(2)
         for a in range(2):
             multiply(3, a)
             largest_apart(3, a)
-        store(1)
+            store_apart(1, a)

@@ -10,7 +10,6 @@ FLOPS = 2 * D * M * E
 
 F32 = mybir.dt.float32
 BF16 = mybir.dt.bfloat16
-I32 = mybir.dt.int32
 U32 = mybir.dt.uint32
 U16 = mybir.dt.uint16
 U8 = mybir.dt.uint8
@@ -35,14 +34,16 @@ def tile_attend_edge_kernel(tc, xT, w, offs, out):
 
     with ExitStack() as ctx:
         keep = ctx.enter_context(tc.tile_pool(name="keep", bufs=1))
+        shared = ctx.enter_context(tc.tile_pool(name="shared", bufs=1))
         psum = ctx.enter_context(tc.psum_pool(name="psum", bufs=1))
 
         lists = keep.tile([P, E // 16], U16, name="lists")
         tables = [keep.tile([P, T], F32, name=f"table{t}") for t in range(4)]
         narrow = [keep.tile([P, T], BF16, name=f"narrow{t}") for t in range(4)]
-        w_raw = keep.tile([P, 4, M], F32, name="w_raw", tag="slot1", align_bytes=64)
-        cols = keep.tile([P, E * 4], BF16, name="cols", align_bytes=64)
-        places = cols[:].rearrange("p (c j) -> p c j", j=4)
+        w_raw = shared.tile([P, 4, M], F32, name="w_raw", offset=0, align_bytes=64)
+        cols = keep.tile([P, (E + M) * 4], BF16, name="cols", align_bytes=64)
+        places = cols[:, 4 * P : 4 * (P + E)].rearrange("p (c j) -> p c j", j=4)
+        w_bf = [cols[:, 4 * (P + E) :], cols[:, : 4 * P]]
 
         for t in LOAD_ORDER:
             for c, n in LAST_CHUNKS if t == 3 else CHUNKS:
@@ -68,94 +69,68 @@ def tile_attend_edge_kernel(tc, xT, w, offs, out):
                     nc.vector.tensor_copy(narrow[t][:, c + n // 96 * 32 : c + n], tables[t][:, c + n // 96 * 32 : c + n])
                 else:
                     nc.vector.tensor_copy(narrow[t][:, c : c + n], tables[t][:, c : c + n])
-            gather_vector(t, 0, SHARE[t])
-            gather_scalar(t, SHARE[t], E - SHARE[t])
+            gather_vector(t, E - SHARE[t], SHARE[t])
+            gather_scalar(t, 0, E - SHARE[t])
         for c, n in LAST_CHUNKS:
             nc.vector.tensor_copy(narrow[3][:, c : c + n], tables[3][:, c : c + n])
-        gather_vector(3, 0, N)
-        for i in range(1, PIECES):
+        gather_vector(3, E - N, N)
+        for i in range(PIECES - 1):
             gather_scalar(3, i * N, N)
-
-        w_bf = [keep.tile([P, P, 4], BF16, name=f"w_bf{a}", tag=f"w_bf{a}", align_bytes=64) for a in range(M // P)]
-        w_codes = keep.tile([P, M], U32, name="w_codes", align_bytes=64)
-        w_scales = keep.tile([P, M], U8, name="w_scales", align_bytes=64)
 
         def cast_w(a):
             nc.vector.tensor_copy(
-                w_bf[a][:].rearrange("p (c i) j -> p c j i", i=4),
+                w_bf[a].rearrange("p (c i j) -> p c j i", i=4, j=4),
                 w_raw[:, :, a * P : (a + 1) * P].rearrange("p j (c i) -> p c j i", i=4),
             )
 
-        def quantize_w(a):
-            nc.vector.quantize_mx(
-                out=w_codes[:, a * P : (a + 1) * P].bitcast(FP8X4),
-                scales=w_scales[:, a * P : (a + 1) * P],
-                in_=w_bf[a][:].rearrange("p m j -> p (m j)"),
-            )
+        def quantize(name, first, n, offset=None):
+            codes = keep.tile([P, n], U32, name=f"codes_{name}", align_bytes=64)
+            if offset is None:
+                scales = keep.tile([P, n], U8, name=f"scales_{name}", align_bytes=64)
+            else:
+                scales = shared.tile([P, n], U8, name=f"scales_{name}", offset=offset, align_bytes=64)
+            nc.vector.quantize_mx(out=codes[:].bitcast(FP8X4), scales=scales[:], in_=cols[:, 4 * first : 4 * (first + n)])
+            return codes, scales
 
-        codes = [keep.tile([P, N], U32, name=f"codes{i}", align_bytes=64) for i in range(PIECES)]
-        scales = [None] * PIECES
-        slots = ["slot1", "w_bf0", "w_bf1", "slot1"]
-        apart = {i: [psum.tile([P, N], F32, name=f"bank{i}_{a}") for a in range(M // P)] for i in (0, PIECES - 1)}
-        sums = {i: psum.tile([P, M // P, N], F32, name=f"bank{i}") for i in range(1, PIECES - 1)}
-
-        def multiply(i, a):
+        def multiply(bank, w_mx, x_mx):
             nc.tensor.matmul_mx(
-                out=apart[i][a][:] if i in apart else sums[i][:, a, :],
-                lhsT=w_codes[:, a * P : (a + 1) * P].bitcast(FP8X4),
-                lhsT_scale=w_scales[:, a * P : (a + 1) * P],
-                rhs=codes[i][:].bitcast(FP8X4),
-                rhs_scale=scales[i][:],
+                out=bank,
+                lhsT=w_mx[0].bitcast(FP8X4),
+                lhsT_scale=w_mx[1],
+                rhs=x_mx[0].bitcast(FP8X4),
+                rhs_scale=x_mx[1],
                 start=True,
                 stop=True,
             )
 
         GH = G // 2
+        GN = N // NB
         ys = [keep.tile([P, M // P, GH], F32, name=f"y{h}") for h in range(2)]
 
-        def largest(i):
-            h, c = divmod(i * N // NB, GH)
-            nc.vector.tensor_reduce(
-                ys[h][:, :, c : c + N // NB], sums[i][:].rearrange("p a (g j) -> p a g j", j=NB), AXIS_X, MAX
-            )
+        def apart(x_mx, y, c, a, name):
+            bank = psum.tile([P, N], F32, name=name)
+            multiply(bank[:], w_mx[a], x_mx)
+            nc.vector.tensor_reduce(y[:, a, c : c + GN], bank[:].rearrange("p (g j) -> p g j", j=NB), AXIS_X, MAX)
 
-        def largest_apart(i, a):
-            h, c = divmod(i * N // NB, GH)
-            nc.vector.tensor_reduce(
-                ys[h][:, a, c : c + N // NB], apart[i][a][:].rearrange("p (g j) -> p g j", j=NB), AXIS_X, MAX
-            )
-
-        def store(h):
-            nc.sync.dma_start(out_rows[:, :, h * GH : (h + 1) * GH], ys[h][:])
-
-        def store_apart(h, a):
-            nc.sync.dma_start(out_rows[:, a, h * GH : (h + 1) * GH], ys[h][:, a, :])
-
-        def quantize(i):
-            scales[i] = keep.tile([P, N], U8, name=f"scales{i}", tag=slots[i], align_bytes=64)
-            nc.vector.quantize_mx(
-                out=codes[i][:].bitcast(FP8X4), scales=scales[i][:], in_=cols[:, 4 * N * i : 4 * N * (i + 1)]
-            )
+        def together(x_mx, y, c, name):
+            bank = psum.tile([P, M // P, N], F32, name=name)
+            for a in range(M // P):
+                multiply(bank[:, a, :], w_mx[a], x_mx)
+            nc.vector.tensor_reduce(y[:, :, c : c + GN], bank[:].rearrange("p a (g j) -> p a g j", j=NB), AXIS_X, MAX)
 
         cast_w(0)
         cast_w(1)
-        quantize_w(0)
-        quantize(0)
-        quantize_w(1)
-        quantize(1)
-        quantize(2)
-        for a in range(2):
-            multiply(0, a)
-            largest_apart(0, a)
-        quantize(3)
-        for a in range(2):
-            multiply(1, a)
-        largest(1)
-        store(0)
-        for a in range(2):
-            multiply(2, a)
-        largest(2)
-        for a in range(2):
-            multiply(3, a)
-            largest_apart(3, a)
-            store_apart(1, a)
+        first = quantize("first", P + E - N, N + P)
+        second = quantize("second", 0, P + N)
+        third = quantize("third", P + N, N, 0)
+        w_mx = [[tile[:, N:] for tile in first], [tile[:, :P] for tile in second]]
+        for a in range(M // P):
+            apart([tile[:, :N] for tile in first], ys[0], 0, a, f"first{a}")
+        nc.sync.dma_start(out_rows[:, :, G - GN : G], ys[0][:, :, 0:GN])
+        fourth = quantize("fourth", P + 2 * N, N, N)
+        together([tile[:, P:] for tile in second], ys[0], GN, "second")
+        nc.sync.dma_start(out_rows[:, :, 0:GN], ys[0][:, :, GN:GH])
+        together([tile[:] for tile in third], ys[1], 0, "third")
+        for a in range(M // P):
+            apart([tile[:] for tile in fourth], ys[1], GN, a, f"fourth{a}")
+            nc.sync.dma_start(out_rows[:, a, GN : GN + GH], ys[1][:, a, :])

@@ -23,7 +23,7 @@ PIECES = E // N
 LOAD_ORDER = [0, 1, 2, 3]
 CHUNKS = [(0, 1408), (1408, 640)]
 LAST_CHUNKS = [(0, 1408), (1408, 640)]
-SHARE = {0: 352, 1: 352, 2: N, 3: N}
+SHARE = {0: 352, 1: 352, 2: 320, 3: N}
 
 
 def tile_attend_edge_kernel(tc, xT, w, offs, out):
@@ -124,11 +124,16 @@ def tile_attend_edge_kernel(tc, xT, w, offs, out):
         second = quantize("second", 0, P + N)
         third = quantize("third", P + N, N, 0)
         w_mx = [[tile[:, N:] for tile in first], [tile[:, :P] for tile in second]]
-        for a in range(M // P):
-            apart([tile[:, :N] for tile in first], ys[0], 0, a, f"first{a}")
-        nc.sync.dma_start(out_rows[:, :, G - GN : G], ys[0][:, :, 0:GN])
+        x3 = [tile[:, :N] for tile in first]
+        x0 = [tile[:, P:] for tile in second]
+        apart(x3, ys[0], 0, 0, "first0")
+        apart(x0, ys[0], GN, 0, "second0")
         fourth = quantize("fourth", P + 2 * N, N, N)
-        together([tile[:, P:] for tile in second], ys[0], GN, "second")
+        bank = psum.tile([P, 2, N], F32, name="both1")
+        multiply(bank[:, 0, :], w_mx[1], x3)
+        multiply(bank[:, 1, :], w_mx[1], x0)
+        nc.vector.tensor_reduce(ys[0][:, 1, :], bank[:].rearrange("p r (g j) -> p (r g) j", j=NB), AXIS_X, MAX)
+        nc.sync.dma_start(out_rows[:, :, G - GN : G], ys[0][:, :, 0:GN])
         nc.sync.dma_start(out_rows[:, :, 0:GN], ys[0][:, :, GN:GH])
         together([tile[:] for tile in third], ys[1], 0, "third")
         for a in range(M // P):

@@ -20,10 +20,12 @@ AXIS_X = mybir.AxisListType.X
 
 N = 256
 PIECES = E // N
-LOAD_ORDER = [0, 1, 2, 3]
-CHUNKS = [(0, 1408), (1408, 640)]
-LAST_CHUNKS = [(0, 1408), (1408, 640)]
-SHARE = {0: 352, 1: 352, 2: 320, 3: N}
+LOAD_ORDER = [2, 0, 1, 3]
+CHUNKS = [(0, T)]
+LAST_CHUNKS = [(0, 1024), (1024, 1024)]
+OWN = 352
+OWN_PIECES = [(0, 160), (160, 192)]
+SPLIT = 640
 
 
 def tile_attend_edge_kernel(tc, xT, w, offs, out):
@@ -39,7 +41,7 @@ def tile_attend_edge_kernel(tc, xT, w, offs, out):
 
         lists = keep.tile([P, E // 16], U16, name="lists")
         tables = [keep.tile([P, T], F32, name=f"table{t}") for t in range(4)]
-        narrow = [keep.tile([P, T], BF16, name=f"narrow{t}") for t in range(4)]
+        narrow = {t: keep.tile([P, T], BF16, name=f"narrow{t}") for t in (LOAD_ORDER[0], LOAD_ORDER[3])}
         w_raw = shared.tile([P, 4, M], F32, name="w_raw", offset=0, align_bytes=64)
         cols = keep.tile([P, (E + M) * 4], BF16, name="cols", align_bytes=64)
         places = cols[:, 4 * P : 4 * (P + E)].rearrange("p (c j) -> p c j", j=4)
@@ -62,17 +64,21 @@ def tile_attend_edge_kernel(tc, xT, w, offs, out):
                 places[:, first : first + n, t], narrow[t][:].indirect(lists[:, first // 16 : (first + n) // 16]), COPY
             )
 
-        for t in LOAD_ORDER[:3]:
-            for c, n in CHUNKS:
-                if t == LOAD_ORDER[0]:
-                    nc.scalar.copy(narrow[t][:, c : c + n // 96 * 32], tables[t][:, c : c + n // 96 * 32])
-                    nc.vector.tensor_copy(narrow[t][:, c + n // 96 * 32 : c + n], tables[t][:, c + n // 96 * 32 : c + n])
-                else:
-                    nc.vector.tensor_copy(narrow[t][:, c : c + n], tables[t][:, c : c + n])
-            gather_vector(t, E - SHARE[t], SHARE[t])
-            gather_scalar(t, 0, E - SHARE[t])
-        for c, n in LAST_CHUNKS:
-            nc.vector.tensor_copy(narrow[3][:, c : c + n], tables[3][:, c : c + n])
+        first_plane, last_plane = LOAD_ORDER[0], LOAD_ORDER[3]
+        half = T // 2
+        nc.scalar.copy(narrow[first_plane][:, :half], tables[first_plane][:, :half])
+        nc.gpsimd.tensor_copy(narrow[first_plane][:, half:], tables[first_plane][:, half:])
+        gather_vector(first_plane, OWN, E - OWN)
+        gather_scalar(first_plane, 0, OWN)
+        for t in LOAD_ORDER[1:3]:
+            gather_vector(t, OWN, E - OWN)
+            for first, n in OWN_PIECES:
+                plain = keep.tile([P, n], BF16, name=f"plain{t}_{first}")
+                nc.scalar.activation(plain[:], tables[t][:].indirect(lists[:, first // 16 : (first + n) // 16]), COPY)
+                nc.gpsimd.tensor_copy(places[:, first : first + n, t], plain[:])
+        nc.scalar.copy(narrow[last_plane][:, :half], tables[last_plane][:, :half])
+        nc.vector.tensor_copy(narrow[last_plane][:, half : half + SPLIT], tables[last_plane][:, half : half + SPLIT])
+        nc.scalar.copy(narrow[last_plane][:, half + SPLIT :], tables[last_plane][:, half + SPLIT :])
         gather_vector(3, E - N, N)
         for i in range(PIECES - 1):
             gather_scalar(3, i * N, N)

@@ -25,7 +25,8 @@ CHUNKS = [(0, T)]
 LAST_CHUNKS = [(0, 1024), (1024, 1024)]
 OWN = 352
 OWN_PIECES = [(0, 160), (160, 192)]
-SPLIT = 640
+SPLIT = 512
+LAST_SHARE = 256
 
 
 def tile_attend_edge_kernel(tc, xT, w, offs, out):
@@ -40,8 +41,8 @@ def tile_attend_edge_kernel(tc, xT, w, offs, out):
         psum = ctx.enter_context(tc.psum_pool(name="psum", bufs=1))
 
         lists = keep.tile([P, E // 16], U16, name="lists")
-        tables = [keep.tile([P, T], F32, name=f"table{t}") for t in range(4)]
-        narrow = {t: keep.tile([P, T], BF16, name=f"narrow{t}") for t in (LOAD_ORDER[0], LOAD_ORDER[3])}
+        tables = [keep.tile([P, T], F32, name=f"table{t}", tag="first" if t == LOAD_ORDER[0] else f"table{t}") for t in range(4)]
+        narrow = {LOAD_ORDER[0]: keep.tile([P, T], BF16, name="narrow_first")}
         w_raw = shared.tile([P, 4, M], F32, name="w_raw", offset=0, align_bytes=64)
         cols = keep.tile([P, (E + M) * 4], BF16, name="cols", align_bytes=64)
         places = cols[:, 4 * P : 4 * (P + E)].rearrange("p (c j) -> p c j", j=4)
@@ -76,12 +77,13 @@ def tile_attend_edge_kernel(tc, xT, w, offs, out):
                 plain = keep.tile([P, n], BF16, name=f"plain{t}_{first}")
                 nc.scalar.activation(plain[:], tables[t][:].indirect(lists[:, first // 16 : (first + n) // 16]), COPY)
                 nc.gpsimd.tensor_copy(places[:, first : first + n, t], plain[:])
+        narrow[last_plane] = keep.tile([P, T], BF16, name="narrow_last", tag="first")
         nc.scalar.copy(narrow[last_plane][:, :half], tables[last_plane][:, :half])
-        nc.vector.tensor_copy(narrow[last_plane][:, half : half + SPLIT], tables[last_plane][:, half : half + SPLIT])
+        nc.gpsimd.tensor_copy(narrow[last_plane][:, half : half + SPLIT], tables[last_plane][:, half : half + SPLIT])
         nc.scalar.copy(narrow[last_plane][:, half + SPLIT :], tables[last_plane][:, half + SPLIT :])
-        gather_vector(3, E - N, N)
-        for i in range(PIECES - 1):
-            gather_scalar(3, i * N, N)
+        gather_vector(3, E - LAST_SHARE, LAST_SHARE)
+        for first in range(0, E - LAST_SHARE, N):
+            gather_scalar(3, first, min(N, E - LAST_SHARE - first))
 
         def cast_w(a):
             nc.vector.tensor_copy(

@@ -20,12 +20,11 @@ AXIS_X = mybir.AxisListType.X
 
 N = 256
 PIECES = E // N
-LOAD_ORDER = [2, 0, 1, 3]
+LOAD_ORDER = [0, 2, 1, 3]
 CHUNKS = [(0, T)]
-LAST_CHUNKS = [(0, 1024), (1024, 1024)]
-OWN = 352
-OWN_PIECES = [(0, 160), (160, 192)]
-SPLIT = 512
+LAST_CHUNKS = [(0, 896), (896, 640), (1536, 512)]
+OWN = {0: 256, 2: 416, 1: 256}
+LAID = 256
 LAST_SHARE = 256
 
 
@@ -41,7 +40,7 @@ def tile_attend_edge_kernel(tc, xT, w, offs, out):
         psum = ctx.enter_context(tc.psum_pool(name="psum", bufs=1))
 
         lists = keep.tile([P, E // 16], U16, name="lists")
-        tables = [keep.tile([P, T], F32, name=f"table{t}", tag="first" if t == LOAD_ORDER[0] else f"table{t}") for t in range(4)]
+        tables = [keep.tile([P, T], F32, name=f"table{t}", tag="second" if t == LOAD_ORDER[1] else f"table{t}") for t in range(4)]
         narrow = {LOAD_ORDER[0]: keep.tile([P, T], BF16, name="narrow_first")}
         w_raw = shared.tile([P, 4, M], F32, name="w_raw", offset=0, align_bytes=64)
         cols = keep.tile([P, (E + M) * 4], BF16, name="cols", align_bytes=64)
@@ -69,18 +68,24 @@ def tile_attend_edge_kernel(tc, xT, w, offs, out):
         half = T // 2
         nc.scalar.copy(narrow[first_plane][:, :half], tables[first_plane][:, :half])
         nc.gpsimd.tensor_copy(narrow[first_plane][:, half:], tables[first_plane][:, half:])
-        gather_vector(first_plane, OWN, E - OWN)
-        gather_scalar(first_plane, 0, OWN)
+        gather_vector(first_plane, OWN[first_plane], E - OWN[first_plane])
+        gather_scalar(first_plane, 0, OWN[first_plane])
         for t in LOAD_ORDER[1:3]:
-            gather_vector(t, OWN, E - OWN)
-            for first, n in OWN_PIECES:
+            gather_vector(t, OWN[t], E - OWN[t])
+            pieces = [(0, LAID // 2, nc.gpsimd.tensor_copy), (LAID // 2, LAID // 2, nc.gpsimd.tensor_copy)]
+            if OWN[t] > LAID:
+                pieces.append((LAID, OWN[t] - LAID, nc.scalar.copy))
+            for first, n, lay in pieces:
                 plain = keep.tile([P, n], BF16, name=f"plain{t}_{first}")
                 nc.scalar.activation(plain[:], tables[t][:].indirect(lists[:, first // 16 : (first + n) // 16]), COPY)
-                nc.gpsimd.tensor_copy(places[:, first : first + n, t], plain[:])
-        narrow[last_plane] = keep.tile([P, T], BF16, name="narrow_last", tag="first")
-        nc.scalar.copy(narrow[last_plane][:, :half], tables[last_plane][:, :half])
-        nc.gpsimd.tensor_copy(narrow[last_plane][:, half : half + SPLIT], tables[last_plane][:, half : half + SPLIT])
-        nc.scalar.copy(narrow[last_plane][:, half + SPLIT :], tables[last_plane][:, half + SPLIT :])
+                lay(places[:, first : first + n, t], plain[:])
+        narrow[last_plane] = keep.tile([P, T], BF16, name="narrow_last", tag="second")
+        c, n = LAST_CHUNKS[0]
+        nc.scalar.copy(narrow[last_plane][:, c : c + n], tables[last_plane][:, c : c + n])
+        for c, n in LAST_CHUNKS[1:]:
+            mid = c + n // 2
+            nc.gpsimd.tensor_copy(narrow[last_plane][:, c:mid], tables[last_plane][:, c:mid])
+            nc.scalar.copy(narrow[last_plane][:, mid : c + n], tables[last_plane][:, mid : c + n])
         gather_vector(3, E - LAST_SHARE, LAST_SHARE)
         for first in range(0, E - LAST_SHARE, N):
             gather_scalar(3, first, min(N, E - LAST_SHARE - first))

@@ -23,8 +23,8 @@ PIECES = E // N
 LOAD_ORDER = [0, 2, 1, 3]
 CHUNKS = [(0, T)]
 LAST_CHUNKS = [(0, 896), (896, 640), (1536, 512)]
-OWN = {0: 256, 2: 416, 1: 256}
-LAID = 256
+OWN = {0: 320, 2: 448, 1: 320}
+LAID = 320
 LAST_SHARE = 256
 
 

from contextlib import ExitStack

import concourse.mybir as mybir

D, T, M = 512, 2048, 256
G, NB = 64, 16
E = G * NB
P = 128
FLOPS = 2 * D * M * E

F32 = mybir.dt.float32
BF16 = mybir.dt.bfloat16
U32 = mybir.dt.uint32
U16 = mybir.dt.uint16
U8 = mybir.dt.uint8
FP8X4 = mybir.dt.float8_e4m3fn_x4
COPY = mybir.ActivationFunctionType.Copy
MAX = mybir.AluOpType.max
AXIS_X = mybir.AxisListType.X

N = 256
PIECES = E // N
LOAD_ORDER = [0, 2, 1, 3]
CHUNKS = [(0, T)]
LAST_CHUNKS = [(0, 896), (896, 640), (1536, 512)]
OWN = {0: 320, 2: 448, 1: 320}
LAID = 320
LAST_SHARE = 256


def tile_attend_edge_kernel(tc, xT, w, offs, out):
    nc = tc.nc
    x_rows = xT.rearrange("(p j) t -> p j t", j=4)
    w_rows = w.rearrange("(p j) m -> p j m", j=4)
    out_rows = out.rearrange("(a p) g -> p a g", p=P)

    with ExitStack() as ctx:
        keep = ctx.enter_context(tc.tile_pool(name="keep", bufs=1))
        shared = ctx.enter_context(tc.tile_pool(name="shared", bufs=1))
        psum = ctx.enter_context(tc.psum_pool(name="psum", bufs=1))

        lists = keep.tile([P, E // 16], U16, name="lists")
        tables = [keep.tile([P, T], F32, name=f"table{t}", tag="second" if t == LOAD_ORDER[1] else f"table{t}") for t in range(4)]
        narrow = {LOAD_ORDER[0]: keep.tile([P, T], BF16, name="narrow_first")}
        w_raw = shared.tile([P, 4, M], F32, name="w_raw", offset=0, align_bytes=64)
        cols = keep.tile([P, (E + M) * 4], BF16, name="cols", align_bytes=64)
        places = cols[:, 4 * P : 4 * (P + E)].rearrange("p (c j) -> p c j", j=4)
        w_bf = [cols[:, 4 * (P + E) :], cols[:, : 4 * P]]

        for t in LOAD_ORDER:
            for c, n in LAST_CHUNKS if t == 3 else CHUNKS:
                nc.sync.dma_start(tables[t][:, c : c + n], x_rows[:, t, c : c + n])
                if t == LOAD_ORDER[0] and c == 0:
                    nc.sync.dma_start(lists[:], offs)
        nc.sync.dma_start(w_raw[:], w_rows)

        def gather_vector(t, first, n):
            nc.vector.tensor_copy(
                places[:, first : first + n, t], tables[t][:].indirect(lists[:, first // 16 : (first + n) // 16])
            )

        def gather_scalar(t, first, n):
            nc.scalar.activation(
                places[:, first : first + n, t], narrow[t][:].indirect(lists[:, first // 16 : (first + n) // 16]), COPY
            )

        first_plane, last_plane = LOAD_ORDER[0], LOAD_ORDER[3]
        half = T // 2
        nc.scalar.copy(narrow[first_plane][:, :half], tables[first_plane][:, :half])
        nc.gpsimd.tensor_copy(narrow[first_plane][:, half:], tables[first_plane][:, half:])
        gather_vector(first_plane, OWN[first_plane], E - OWN[first_plane])
        gather_scalar(first_plane, 0, OWN[first_plane])
        for t in LOAD_ORDER[1:3]:
            gather_vector(t, OWN[t], E - OWN[t])
            pieces = [(0, LAID // 2, nc.gpsimd.tensor_copy), (LAID // 2, LAID // 2, nc.gpsimd.tensor_copy)]
            if OWN[t] > LAID:
                pieces.append((LAID, OWN[t] - LAID, nc.scalar.copy))
            for first, n, lay in pieces:
                plain = keep.tile([P, n], BF16, name=f"plain{t}_{first}")
                nc.scalar.activation(plain[:], tables[t][:].indirect(lists[:, first // 16 : (first + n) // 16]), COPY)
                lay(places[:, first : first + n, t], plain[:])
        narrow[last_plane] = keep.tile([P, T], BF16, name="narrow_last", tag="second")
        c, n = LAST_CHUNKS[0]
        nc.scalar.copy(narrow[last_plane][:, c : c + n], tables[last_plane][:, c : c + n])
        for c, n in LAST_CHUNKS[1:]:
            mid = c + n // 2
            nc.gpsimd.tensor_copy(narrow[last_plane][:, c:mid], tables[last_plane][:, c:mid])
            nc.scalar.copy(narrow[last_plane][:, mid : c + n], tables[last_plane][:, mid : c + n])
        gather_vector(3, E - LAST_SHARE, LAST_SHARE)
        for first in range(0, E - LAST_SHARE, N):
            gather_scalar(3, first, min(N, E - LAST_SHARE - first))

        def cast_w(a):
            nc.vector.tensor_copy(
                w_bf[a].rearrange("p (c i j) -> p c j i", i=4, j=4),
                w_raw[:, :, a * P : (a + 1) * P].rearrange("p j (c i) -> p c j i", i=4),
            )

        def quantize(name, first, n, offset=None):
            codes = keep.tile([P, n], U32, name=f"codes_{name}", align_bytes=64)
            if offset is None:
                scales = keep.tile([P, n], U8, name=f"scales_{name}", align_bytes=64)
            else:
                scales = shared.tile([P, n], U8, name=f"scales_{name}", offset=offset, align_bytes=64)
            nc.vector.quantize_mx(out=codes[:].bitcast(FP8X4), scales=scales[:], in_=cols[:, 4 * first : 4 * (first + n)])
            return codes, scales

        def multiply(bank, w_mx, x_mx):
            nc.tensor.matmul_mx(
                out=bank,
                lhsT=w_mx[0].bitcast(FP8X4),
                lhsT_scale=w_mx[1],
                rhs=x_mx[0].bitcast(FP8X4),
                rhs_scale=x_mx[1],
                start=True,
                stop=True,
            )

        GH = G // 2
        GN = N // NB
        ys = [keep.tile([P, M // P, GH], F32, name=f"y{h}") for h in range(2)]

        def apart(x_mx, y, c, a, name):
            bank = psum.tile([P, N], F32, name=name)
            multiply(bank[:], w_mx[a], x_mx)
            nc.vector.tensor_reduce(y[:, a, c : c + GN], bank[:].rearrange("p (g j) -> p g j", j=NB), AXIS_X, MAX)

        def together(x_mx, y, c, name):
            bank = psum.tile([P, M // P, N], F32, name=name)
            for a in range(M // P):
                multiply(bank[:, a, :], w_mx[a], x_mx)
            nc.vector.tensor_reduce(y[:, :, c : c + GN], bank[:].rearrange("p a (g j) -> p a g j", j=NB), AXIS_X, MAX)

        cast_w(0)
        cast_w(1)
        first = quantize("first", P + E - N, N + P)
        second = quantize("second", 0, P + N)
        third = quantize("third", P + N, N, 0)
        w_mx = [[tile[:, N:] for tile in first], [tile[:, :P] for tile in second]]
        x3 = [tile[:, :N] for tile in first]
        x0 = [tile[:, P:] for tile in second]
        apart(x3, ys[0], 0, 0, "first0")
        apart(x0, ys[0], GN, 0, "second0")
        fourth = quantize("fourth", P + 2 * N, N, N)
        bank = psum.tile([P, 2, N], F32, name="both1")
        multiply(bank[:, 0, :], w_mx[1], x3)
        multiply(bank[:, 1, :], w_mx[1], x0)
        nc.vector.tensor_reduce(ys[0][:, 1, :], bank[:].rearrange("p r (g j) -> p (r g) j", j=NB), AXIS_X, MAX)
        nc.sync.dma_start(out_rows[:, :, G - GN : G], ys[0][:, :, 0:GN])
        nc.sync.dma_start(out_rows[:, :, 0:GN], ys[0][:, :, GN:GH])
        together([tile[:] for tile in third], ys[1], 0, "third")
        for a in range(M // P):
            apart([tile[:] for tile in fourth], ys[1], GN, a, f"fourth{a}")
            nc.sync.dma_start(out_rows[:, a, GN : GN + GH], ys[1][:, a, :])
